import numpy as np, ml_dtypes
CORES = [125,127,253,255,381,383,509,511]
N = 8
KT, FB, TK = 1, 32, 256
def setup_inputs(rng):
    return {"x": rng.standard_normal((N, 128, KT * TK), dtype=np.float32).astype(ml_dtypes.bfloat16), "w": rng.standard_normal((N, 128, KT * N * FB), dtype=np.float32).astype(ml_dtypes.bfloat16)}
def setup_inputs_big(rng):
    d = setup_inputs(rng)
    for k in ("x", "w"): d[k] = (d[k].astype(np.float32) * 1024.0).astype(d[k].dtype)
    return d
def setup_inputs_small(rng):
    d = setup_inputs(rng)
    for k in ("x", "w"): d[k] = (d[k].astype(np.float32) * (1 / 1024.0)).astype(d[k].dtype)
    return d
def setup_inputs_apart(rng):
    d = setup_inputs(rng)
    f = (10.0 ** rng.permutation(np.linspace(-1.5, 1.5, N))).astype(np.float32).reshape(N, 1, 1)
    for k in ("x", "w"): d[k] = (d[k].astype(np.float32) * f).astype(d[k].dtype)
    return d
def reference(x, w):
    X, W = x.astype(np.float64), w.astype(np.float64)
    y = np.zeros((N, FB, N * TK))
    for j in range(N):
        for r in range(N):
            for t in range(KT):
                y[r][:, TK * j:TK * j + TK] += W[j][:, FB * (N * t + r):FB * (N * t + r) + FB].T @ X[j][:, TK * t:TK * t + TK]
    return {"y": y.astype(ml_dtypes.bfloat16 if x.dtype != np.float64 else np.float64)}

from concourse.bass import DstId, RemoteDMATransfer

N, FB, TK = 8, 32, 256
BW = FB * TK // 128

SCRATCH = {
    "xs": ("sbuf", [128, TK], "bfloat16"),
    "ws": ("sbuf", [128, N * FB], "bfloat16"),
    "ex": ("sbuf", [128, 264], "bfloat16"),
    "pd": ("psum", [128, 512], "float32"),
    "po": ("psum", [128, 512], "float32"),
    "pc": ("psum", [128, 512], "float32"),
    "td": ("sbuf", [128, 2 * BW], "bfloat16"),
    "to": ("sbuf", [128, TK], "bfloat16"),
    "tc": ("sbuf", [128, TK], "bfloat16"),
    "stage": ("dram", [5, 128, BW], "bfloat16"),
    "relay": ("dram", [2, 128, BW], "bfloat16"),
    "land": ("dram", [N, 128, BW], "bfloat16"),
}
SEMAPHORES = ["ldx", "ldw", "zed", "spread", "mmd", "cpd", "mmo", "cpo", "mmc", "cpc", "staged", "rel", "sent", "stored"] + [
    "arr%d" % j for j in range(N)]


def _bits(mask):
    return [b for b in range(16) if (mask >> b) & 1]


def _mask(engines):
    m = 0
    for b in engines:
        m |= 1 << b
    return m


def _place(T, topo, c):
    same = [d for d in T.cores if topo.host(d) == topo.host(c) and topo.chip(d) == topo.chip(c)]
    return same.index(c)


def _routes(T, topo):
    out = []
    for js, s in enumerate(T.cores):
        far = [r for r, d in enumerate(T.cores) if not topo.may_write(s, d)]
        for i, r in enumerate(far):
            d = T.cores[r]
            via = [v for v in T.cores if topo.may_write(s, v) and topo.may_write(v, d)
                   and topo.host(v) != topo.host(s) and _place(T, topo, v) == _place(T, topo, s)]
            via.sort(key=lambda v: 0 if topo.same_plane(s, v) else 1)
            v = via[(i + _place(T, topo, s)) % len(via)]
            out.append((js, r, v, 0 if topo.same_plane(s, v) else 1))
    return out


def rank_program(g, core, T, topo):
    me = T.rank_of(core)
    if me is None:
        return
    S = T.sem
    cores = T.cores

    chipm = [r for r, c in enumerate(cores) if topo.host(c) == topo.host(core) and topo.chip(c) == topo.chip(core)]
    plane = [r for r, c in enumerate(cores) if topo.same_plane(core, c)]
    diag = [r for r, c in enumerate(cores) if not topo.may_write(core, c)]
    cable = [r for r in range(N) if r not in chipm and r not in plane and r not in diag]
    peers = [r for r in chipm if r != me]
    routes = _routes(T, topo)

    def engines(dst):
        b = _bits(topo.mask(core, dst))
        return b[0::2] if topo.same_plane(core, dst) else b[1::2]

    def xfer(dst, eng, sem, src, out):
        rid, pid = topo.addr(dst, core)
        return RemoteDMATransfer(dst_ids=[DstId(rid=rid, pnc=pid)], dma_engine_mask=_mask(eng), remote_sem=sem,
                                 src=src, dst=out)

    def wcols(ranks):
        assert ranks == list(range(ranks[0], ranks[0] + len(ranks)))
        return T.ws[:, FB * ranks[0]: FB * (ranks[-1] + 1)]

    g.vector.memset(T.ex[:, :], 0.0).then_inc(S.zed, 1)
    g.scalar.dma_start(T.ws[:, :], T.w[:, :]).then_inc(S.ldw, 16)
    g.sync.dma_start(T.xs[:, :], T.x[:, :]).then_inc(S.ldx, 16)

    nd = len(diag) * FB
    g.vector.wait_ge(S.zed, 1)
    g.vector.wait_ge(S.ldw, 16)
    g.vector.tensor_copy(T.ex[:, 3:3 + 4 * nd:4], wcols(diag)).then_inc(S.spread, 1)

    g.tensor.wait_ge(S.ldx, 16)
    g.tensor.wait_ge(S.ldw, 16)
    g.tensor.wait_ge(S.spread, 1)
    for d in range(len(diag)):
        for q in range(4):
            o = 128 * d + 3 - q
            mm = g.tensor.matmul(T.pd[:, BW * d:BW * (d + 1)], T.ex[:, o:o + 128], T.xs[:, BW * q:BW * (q + 1)],
                                 start=(q == 0), stop=(q == 3))
        mm.then_inc(S.mmd, 1)
    g.tensor.matmul(T.po[0:64, 0:TK], wcols(plane), T.xs[:, :], start=True, stop=True).then_inc(S.mmo, 1)
    g.tensor.matmul(T.po[64:128, 0:TK], wcols(cable), T.xs[:, :], start=True, stop=True).then_inc(S.mmo, 1)
    g.tensor.matmul(T.pc[0:64, 0:TK], wcols(chipm), T.xs[:, :], start=True, stop=True).then_inc(S.mmc, 1)

    g.vector.wait_ge(S.mmd, len(diag))
    g.vector.tensor_copy(T.td[:, :], T.pd[:, 0:2 * BW]).then_inc(S.cpd, 1)
    g.vector.wait_ge(S.mmo, 2)
    g.vector.tensor_copy(T.to[:, :], T.po[:, 0:TK]).then_inc(S.cpo, 1)
    g.vector.wait_ge(S.mmc, 1)
    g.vector.tensor_copy(T.tc[0:64, :], T.pc[0:64, 0:TK]).then_inc(S.cpc, 1)

    sent = 0
    call = []
    for (js, r, v, slot) in routes:
        if js == me:
            e = engines(v)
            call.append(xfer(v, e, S.rel, T.td[:, BW * diag.index(r):BW * (diag.index(r) + 1)], T.relay[slot]))
            sent += len(e)
    g.wait_ge(S.cpd, 1)
    g.remote_dma_fused(call, local_sem=S.sent)

    g.sync.wait_ge(S.cpo, 1)
    g.sync.dma_start(T.stage[0:4], T.to[:, :]).then_inc(S.staged, 16)
    g.scalar.wait_ge(S.cpc, 1)
    pi = chipm.index(peers[0])
    g.scalar.dma_start(T.stage[4], T.tc[FB * pi:FB * (pi + 1), :]).then_inc(S.staged, 16)
    mi = chipm.index(me)
    g.scalar.dma_start(T.y[:, TK * me:TK * (me + 1)], T.tc[FB * mi:FB * (mi + 1), :]).then_inc(S.stored, 16)
    stores = 1

    arrive = {}
    call = []
    for k, r in enumerate(plane + cable):
        e = engines(cores[r])
        e = e[0:2] if k % 2 == 0 else e[2:4]
        call.append(xfer(cores[r], e, S["arr%d" % me], T.stage[k], T.land[me]))
        sent += len(e)
        arrive[r] = len(e)
    off = _bits(topo.mask(core, cores[plane[0]]))
    on = [b for b in _bits(topo.mask(core, cores[peers[0]])) if b not in off][0:2]
    call.append(xfer(cores[peers[0]], on, S["arr%d" % me], T.stage[4], T.land[me]))
    sent += len(on)
    arrive[peers[0]] = len(on)
    g.wait_ge(S.staged, 32)
    g.remote_dma_fused(call, local_sem=S.sent)

    call = []
    got = 0
    for (js, r, v, slot) in routes:
        if v == core:
            got += len(engines(cores[js]))
            e = engines(cores[r])
            call.append(xfer(cores[r], e, S["arr%d" % js], T.relay[slot], T.land[js]))
            sent += len(e)
        if r == me:
            b = _bits(topo.mask(v, core))
            arrive[js] = len(b[0::2] if topo.same_plane(v, core) else b[1::2])
    g.wait_ge(S.rel, got)
    g.remote_dma_fused(call, local_sem=S.sent)

    order = [peers[0], plane[0], plane[1], cable[0], cable[1], diag[0], diag[1]]
    queues = [g.scalar, g.sync, g.scalar, g.sync, g.scalar, g.sync, g.scalar]
    for j, qu in zip(order, queues):
        qu.wait_ge(S["arr%d" % j], arrive[j])
        qu.dma_start(T.y[:, TK * j:TK * (j + 1)], T.land[j]).then_inc(S.stored, 16)
        stores += 1

    g.wait_ge(S.sent, sent)
    g.wait_ge(S.stored, 16 * stores)
